import numpy as np
import ml_dtypes


def mxq(x, axis, fmt="e4m3"):
    dtype, down = {"e4m3": (ml_dtypes.float8_e4m3fn, 7), "e5m2": (ml_dtypes.float8_e5m2, 14)}[fmt]
    v = np.moveaxis(np.asarray(x, np.float32).astype(ml_dtypes.bfloat16).astype(np.float64), axis, -1)
    blocks = v.reshape(v.shape[:-1] + (-1, 32))
    amax = np.abs(blocks).max(-1, keepdims=True)
    byte = np.maximum(np.where(amax > 0, np.frexp(amax)[1] - 1 + 127, 0) - down, 1)
    scale = np.exp2(byte - 127.0)
    codes = (blocks / scale).astype(np.float32).astype(dtype).astype(np.float64)
    return np.moveaxis((codes * scale).reshape(v.shape), -1, axis)


WIDE = False


def mx_kscale(k):
    if not WIDE:
        return np.ones(k)
    levels = np.array([10, -10, 5, -5, 0])
    if k % 512:
        return np.exp2(np.random.permutation(np.resize(levels, k // 32))).repeat(32)
    a = np.empty((k // 512, 16))
    for p in range(k // 512):
        a[p, :8] = np.random.permutation(np.resize(levels, 8))
        for g in range(8):
            far = levels[np.abs(levels - a[p, g]) >= 10]
            a[p, g + 8] = far[np.random.randint(len(far))]
    return np.exp2(a.ravel()).repeat(32)


def f64(x):
    return np.asarray(x).astype(np.float64)


def striped(idx):
    return np.tile(np.asarray(idx).reshape(-1, 16).T, (8, 1)).astype(np.uint16)


def unstriped(offs):
    return offs[:16].T.reshape(-1).astype(np.int64)


E2M1 = np.array([0.0, 0.5, 1.0, 1.5, 2.0, 3.0, 4.0, 6.0, -0.0, -0.5, -1.0, -1.5, -2.0, -3.0, -4.0, -6.0])


def pack_weight(w, fmt):
    k, n = w.shape
    w = f64(np.asarray(w, np.float32).astype(ml_dtypes.bfloat16)).reshape(k // 32, 32, n)
    amax = np.abs(w).max(1)
    if fmt == "e4m3":
        byte = np.frexp(amax)[1] - 1 + 127 - 7
    else:
        mant, ex = np.frexp(amax / 6.0)
        byte = np.where(mant > 0.5, ex, ex - 1) + 127
    byte = np.clip(np.where(amax > 0, byte, 1), 1, 254)
    scaled = (w * np.exp2(127.0 - byte)[:, None, :]).reshape(k, n).astype(np.float32)
    by_word = np.ascontiguousarray(scaled.reshape(k // 512, 128, 4, n).transpose(0, 1, 3, 2))
    if fmt == "e4m3":
        words = by_word.astype(ml_dtypes.float8_e4m3fn).view(np.uint8)
    else:
        c = by_word.astype(ml_dtypes.float4_e2m1fn).view(np.uint8) & 0xF
        words = (c[..., 0::2] | (c[..., 1::2] << 4)).reshape(k // 512, 128, 2 * n)
    return np.ascontiguousarray(words), np.ascontiguousarray(byte.astype(np.uint8).reshape(k // 512, 16, n))


def unpack_weight(words, scales, fmt):
    g, _, n = scales.shape
    words = np.ascontiguousarray(words).reshape(g, 128, n, -1)
    if fmt == "e4m3":
        vals = words.view(ml_dtypes.float8_e4m3fn).astype(np.float64)
    else:
        nib = np.empty((g, 128, n, 4), np.uint8)
        nib[..., 0::2] = words & 0xF
        nib[..., 1::2] = words >> 4
        vals = E2M1[nib]
    vals = vals * np.repeat(np.exp2(scales.astype(np.float64) - 127.0), 8, axis=1)[..., None]
    return vals.transpose(0, 1, 3, 2).reshape(g * 512, n)


def silu(v):
    return v / (1.0 + np.exp(-v))


B, N, T, D, NQ = 1, 512, 2048, 512, 128


def setup_inputs():
    n = np.random.standard_normal
    idx = np.sort(np.random.permutation(T)[:B * N].reshape(B, N), axis=1).reshape(-1)
    s = mx_kscale(D)[:, None]
    kp = pack_weight(n((D, T)) / s, "e4m3")
    cp = pack_weight(n((D, T)) / s, "e4m3")
    return {
        "qT": (n((B, D, NQ)) * s * (1.00 / np.sqrt(D))).astype(np.float32),
        "k_words": kp[0],
        "k_scales": kp[1],
        "c_words": cp[0],
        "c_scales": cp[1],
        "offs": striped(idx),
    }


def reference(qT, k_words, k_scales, c_words, c_scales, offs):
    idx = unstriped(offs)
    pick = lambda x, which: x[:, which].reshape(x.shape[0], B, -1).transpose(1, 0, 2)
    k = unpack_weight(k_words, k_scales, "e4m3")
    kg = pick(k, idx)
    c = unpack_weight(c_words, c_scales, "e4m3")
    cg = pick(c, idx)
    qq = mxq(f64(qT), 1, "e4m3")
    a = qq.transpose(0, 2, 1) @ kg
    z = qq.transpose(0, 2, 1) @ cg
    y = silu(a) * z
    return y

@@ -1,0 +1,99 @@
+from contextlib import ExitStack
+
+import concourse.mybir as mybir
+
+T, N, D, NQ = 2048, 512, 512, 128
+FLOPS = 2 * 2 * D * NQ * N
+
+F32 = mybir.dt.float32
+BF16 = mybir.dt.bfloat16
+I32 = mybir.dt.int32
+U32 = mybir.dt.uint32
+U16 = mybir.dt.uint16
+U8 = mybir.dt.uint8
+FP8X4 = mybir.dt.float8_e4m3fn_x4
+
+P = 128
+PACK = 4
+HALF = N // 2
+C_ROW = 4
+
+
+def tile_attend_neu_swiglu_srt_kernel(tc, qT, k_words, k_scales, c_words, c_scales, offs, out):
+    nc = tc.nc
+    with ExitStack() as ctx:
+        pool = ctx.enter_context(tc.tile_pool(name="sbuf", bufs=1))
+        psum = ctx.enter_context(tc.psum_pool(name="psum", bufs=1))
+
+        offsets = pool.tile([P, N // 16], U16, name="offsets")
+        k_table = pool.tile([P, T], I32, name="k_table", align_bytes=64)
+        c_table = pool.tile([P, T], I32, name="c_table", align_bytes=64)
+        k_plane = pool.tile([P, T], U8, name="k_plane", tag="k_slot", align_bytes=64)
+        c_plane = pool.tile([P, T], U8, name="c_plane", tag="c_slot", align_bytes=64)
+        q_raw = pool.tile([P, PACK, NQ], F32, name="q_raw", align_bytes=64)
+
+        def words(dram):
+            return dram[0].rearrange("p t r -> p (t r)").bitcast(I32)
+
+        def load_rows(queue, plane, row, scales, quad):
+            queue.dma_start(
+                plane[32 * quad + row : 32 * quad + row + 4, :].bitcast(I32),
+                scales[0, 4 * quad : 4 * quad + 4, :].bitcast(I32),
+            )
+
+        nc.sync.dma_start(offsets[:], offs)
+        nc.scalar.dma_start(q_raw[:], qT[0].rearrange("(p j) q -> p j q", j=PACK))
+        nc.scalar.dma_start(k_table[:], words(k_words))
+        nc.scalar.dma_start(c_table[:], words(c_words))
+
+        nc.vector.memset(c_plane[:].bitcast(I32), 0)
+        nc.vector.memset(k_plane[:].bitcast(I32), 0)
+        for quad in range(2, 4):
+            load_rows(nc.gpsimd, c_plane, C_ROW, c_scales, quad)
+        for quad in range(4):
+            load_rows(nc.sync, k_plane, 0, k_scales, quad)
+        for quad in range(2):
+            load_rows(nc.sync, c_plane, C_ROW, c_scales, quad)
+
+        q_grouped = pool.tile([P, NQ, PACK], BF16, name="q_grouped", align_bytes=64)
+        q_codes = pool.tile([P, NQ], U32, name="q_codes", align_bytes=64)
+        q_plane = pool.tile([P, NQ], U8, name="q_plane", align_bytes=64)
+        nc.vector.tensor_copy(out=q_grouped[:], in_=q_raw[:].rearrange("p j q -> p q j"))
+        k_bytes = pool.tile([P, N], U8, name="k_bytes", align_bytes=64)
+        nc.vector.tensor_copy(k_bytes[:], k_plane[:].indirect(offsets[:]))
+        nc.vector.quantize_mx(
+            out=q_codes[:].bitcast(FP8X4), scales=q_plane[:], in_=q_grouped[:].rearrange("p q j -> p (q j)")
+        )
+
+        def product(name, table, picked, picked_bytes, row, h):
+            cols = slice(h * HALF, (h + 1) * HALF)
+            nc.vector.tensor_copy(picked[:, cols], table[:].bitcast(U32).indirect(offsets[:, h * HALF // 16 : (h + 1) * HALF // 16]))
+            acc = psum.tile([NQ, HALF], F32, name=name + "_acc%d" % h)
+            nc.tensor.matmul_mx(
+                out=acc[:],
+                lhsT=q_codes[:].bitcast(FP8X4),
+                lhsT_scale=q_plane[:],
+                rhs=picked[:, cols].bitcast(FP8X4),
+                rhs_scale=picked_bytes[row:P, cols],
+                start=True,
+                stop=True,
+            )
+            return acc
+
+        gates = []
+        k_picked = pool.tile([P, N], U32, name="k_picked", tag="k_slot", align_bytes=64)
+        for h in range(2):
+            acc = product("k", k_table, k_picked, k_bytes, 0, h)
+            gate = pool.tile([NQ, HALF], F32, name="gate%d" % h)
+            nc.scalar.activation(gate[:], acc[:], mybir.ActivationFunctionType.Silu)
+            gates.append(gate)
+
+        c_bytes = pool.tile([P, N], U8, name="c_bytes", align_bytes=64)
+        nc.vector.tensor_copy(c_bytes[:], c_plane[:].indirect(offsets[:]))
+        c_picked = pool.tile([P, N], U32, name="c_picked", tag="c_slot", align_bytes=64)
+        layers = [product("c", c_table, c_picked, c_bytes, C_ROW, h) for h in range(2)]
+        for h in range(2):
+            result = pool.tile([NQ, HALF], F32, name="result%d" % h)
+            nc.vector.tensor_tensor(result[:], layers[h][:], gates[h][:], mybir.AluOpType.mult)
+            queue = nc.sync if h == 0 else nc.scalar
+            queue.dma_start(out[0, :, h * HALF : (h + 1) * HALF], result[:])

@@ -41,19 +41,16 @@ def tile_attend_neu_swiglu_srt_kernel(tc, qT, k_words, k_scales, c_words, c_scal
                 scales[0, 4 * quad : 4 * quad + 4, :].bitcast(I32),
             )
 
-        nc.sync.dma_start(offsets[:], offs)
-        nc.scalar.dma_start(q_raw[:], qT[0].rearrange("(p j) q -> p j q", j=PACK))
-        nc.scalar.dma_start(k_table[:], words(k_words))
-        nc.scalar.dma_start(c_table[:], words(c_words))
-
-        nc.vector.memset(c_plane[:].bitcast(I32), 0)
         nc.vector.memset(k_plane[:].bitcast(I32), 0)
-        for quad in range(2, 4):
-            load_rows(nc.gpsimd, c_plane, C_ROW, c_scales, quad)
+        nc.vector.memset(c_plane[:].bitcast(I32), 0)
+        nc.sync.dma_start(offsets[:], offs)
+        nc.sync.dma_start(q_raw[:], qT[0].rearrange("(p j) q -> p j q", j=PACK))
         for quad in range(4):
             load_rows(nc.sync, k_plane, 0, k_scales, quad)
-        for quad in range(2):
+        nc.sync.dma_start(k_table[:], words(k_words))
+        for quad in range(4):
             load_rows(nc.sync, c_plane, C_ROW, c_scales, quad)
+        nc.sync.dma_start(c_table[:], words(c_words))
 
         q_grouped = pool.tile([P, NQ, PACK], BF16, name="q_grouped", align_bytes=64)
         q_codes = pool.tile([P, NQ], U32, name="q_codes", align_bytes=64)

@@ -17,6 +17,7 @@ P = 128
 PACK = 4
 HALF = N // 2
 C_ROW = 4
+REACH = T - HALF
 
 
 def tile_attend_neu_swiglu_srt_kernel(tc, qT, k_words, k_scales, c_words, c_scales, offs, out):
@@ -35,22 +36,20 @@ def tile_attend_neu_swiglu_srt_kernel(tc, qT, k_words, k_scales, c_words, c_scal
         def words(dram):
             return dram[0].rearrange("p t r -> p (t r)").bitcast(I32)
 
-        def load_rows(queue, plane, row, scales, quad):
-            queue.dma_start(
-                plane[32 * quad + row : 32 * quad + row + 4, :].bitcast(I32),
-                scales[0, 4 * quad : 4 * quad + 4, :].bitcast(I32),
-            )
+        def load_rows(plane, row, scales, r):
+            nc.sync.dma_start(plane[row + r : P : 32, :].bitcast(I32), scales[0, r : 16 : 4, :].bitcast(I32))
 
         nc.vector.memset(k_plane[:].bitcast(I32), 0)
         nc.vector.memset(c_plane[:].bitcast(I32), 0)
         nc.sync.dma_start(offsets[:], offs)
         nc.sync.dma_start(q_raw[:], qT[0].rearrange("(p j) q -> p j q", j=PACK))
-        for quad in range(4):
-            load_rows(nc.sync, k_plane, 0, k_scales, quad)
+        for r in range(4):
+            load_rows(k_plane, 0, k_scales, r)
         nc.sync.dma_start(k_table[:], words(k_words))
-        for quad in range(4):
-            load_rows(nc.sync, c_plane, C_ROW, c_scales, quad)
-        nc.sync.dma_start(c_table[:], words(c_words))
+        for r in range(4):
+            load_rows(c_plane, C_ROW, c_scales, r)
+        nc.sync.dma_start(c_table[:, :REACH], words(c_words)[:, :REACH])
+        nc.sync.dma_start(c_table[:, REACH:], words(c_words)[:, REACH:])
 
         q_grouped = pool.tile([P, NQ, PACK], BF16, name="q_grouped", align_bytes=64)
         q_codes = pool.tile([P, NQ], U32, name="q_codes", align_bytes=64)
@@ -64,7 +63,7 @@ def tile_attend_neu_swiglu_srt_kernel(tc, qT, k_words, k_scales, c_words, c_scal
 
         def product(name, table, picked, picked_bytes, row, h):
             cols = slice(h * HALF, (h + 1) * HALF)
-            nc.vector.tensor_copy(picked[:, cols], table[:].bitcast(U32).indirect(offsets[:, h * HALF // 16 : (h + 1) * HALF // 16]))
+            nc.vector.tensor_copy(picked[:, cols], table[:, : (REACH, T)[h]].bitcast(U32).indirect(offsets[:, h * HALF // 16 : (h + 1) * HALF // 16]))
             acc = psum.tile([NQ, HALF], F32, name=name + "_acc%d" % h)
             nc.tensor.matmul_mx(
                 out=acc[:],

@@ -17,6 +17,7 @@ P = 128
 PACK = 4
 HALF = N // 2
 C_ROW = 4
+SPREAD = 8
 REACH = T - HALF
 
 
@@ -36,27 +37,39 @@ def tile_attend_neu_swiglu_srt_kernel(tc, qT, k_words, k_scales, c_words, c_scal
         def words(dram):
             return dram[0].rearrange("p t r -> p (t r)").bitcast(I32)
 
-        def load_rows(plane, row, scales, r):
-            nc.sync.dma_start(plane[row + r : P : 32, :].bitcast(I32), scales[0, r : 16 : 4, :].bitcast(I32))
+        def load_rows(plane, row, scales):
+            nc.sync.dma_start(plane[row : P : SPREAD, :].bitcast(I32), scales[0].bitcast(I32))
 
+        def pick_rows(name, plane, row):
+            picked = pool.tile([P, N], U8, name=name + "_spread", align_bytes=64)
+            placed = pool.tile([P, N], U8, name=name + "_bytes", align_bytes=64)
+            nc.vector.tensor_copy(picked[:], plane[:].indirect(offsets[:]))
+            nc.vector.tensor_copy(placed[:].bitcast(I32), picked[:].bitcast(I32))
+            for r in range(1, 4):
+                nc.scalar.dma_start(
+                    placed[row + r : P : 32, :].bitcast(I32), picked[row + SPREAD * r : P : 32, :].bitcast(I32)
+                )
+            return placed
+
+        warm = pool.tile([P, 2], F32, name="warm")
+        nc.gpsimd.memset(warm[:, 0:1], 0.0)
+        nc.scalar.activation(warm[:, 1:2], warm[:, 0:1], mybir.ActivationFunctionType.Silu)
         nc.vector.memset(k_plane[:].bitcast(I32), 0)
         nc.vector.memset(c_plane[:].bitcast(I32), 0)
         nc.sync.dma_start(offsets[:], offs)
         nc.sync.dma_start(q_raw[:], qT[0].rearrange("(p j) q -> p j q", j=PACK))
-        for r in range(4):
-            load_rows(k_plane, 0, k_scales, r)
+        load_rows(k_plane, 0, k_scales)
+        load_rows(c_plane, C_ROW, c_scales)
         nc.sync.dma_start(k_table[:], words(k_words))
-        for r in range(4):
-            load_rows(c_plane, C_ROW, c_scales, r)
         nc.sync.dma_start(c_table[:, :REACH], words(c_words)[:, :REACH])
         nc.sync.dma_start(c_table[:, REACH:], words(c_words)[:, REACH:])
 
         q_grouped = pool.tile([P, NQ, PACK], BF16, name="q_grouped", align_bytes=64)
         q_codes = pool.tile([P, NQ], U32, name="q_codes", align_bytes=64)
         q_plane = pool.tile([P, NQ], U8, name="q_plane", align_bytes=64)
-        nc.vector.tensor_copy(out=q_grouped[:], in_=q_raw[:].rearrange("p j q -> p q j"))
-        k_bytes = pool.tile([P, N], U8, name="k_bytes", align_bytes=64)
-        nc.vector.tensor_copy(k_bytes[:], k_plane[:].indirect(offsets[:]))
+        nc.scalar.copy(out=q_grouped[:], in_=q_raw[:].rearrange("p j q -> p q j"))
+        k_bytes = pick_rows("k", k_plane, 0)
+        c_bytes = pick_rows("c", c_plane, C_ROW)
         nc.vector.quantize_mx(
             out=q_codes[:].bitcast(FP8X4), scales=q_plane[:], in_=q_grouped[:].rearrange("p q j -> p (q j)")
         )
@@ -84,8 +97,6 @@ def tile_attend_neu_swiglu_srt_kernel(tc, qT, k_words, k_scales, c_words, c_scal
             nc.scalar.activation(gate[:], acc[:], mybir.ActivationFunctionType.Silu)
             gates.append(gate)
 
-        c_bytes = pool.tile([P, N], U8, name="c_bytes", align_bytes=64)
-        nc.vector.tensor_copy(c_bytes[:], c_plane[:].indirect(offsets[:]))
         c_picked = pool.tile([P, N], U32, name="c_picked", tag="c_slot", align_bytes=64)
         layers = [product("c", c_table, c_picked, c_bytes, C_ROW, h) for h in range(2)]
         for h in range(2):

@@ -17,7 +17,7 @@ P = 128
 PACK = 4
 HALF = N // 2
 C_ROW = 4
-SPREAD = 8
+TOP = 112
 REACH = T - HALF
 
 
@@ -37,29 +37,19 @@ def tile_attend_neu_swiglu_srt_kernel(tc, qT, k_words, k_scales, c_words, c_scal
         def words(dram):
             return dram[0].rearrange("p t r -> p (t r)").bitcast(I32)
 
-        def load_rows(plane, row, scales):
-            nc.sync.dma_start(plane[row : P : SPREAD, :].bitcast(I32), scales[0].bitcast(I32))
-
-        def pick_rows(name, plane, row):
-            picked = pool.tile([P, N], U8, name=name + "_spread", align_bytes=64)
-            placed = pool.tile([P, N], U8, name=name + "_bytes", align_bytes=64)
-            nc.vector.tensor_copy(picked[:], plane[:].indirect(offsets[:]))
-            nc.vector.tensor_copy(placed[:].bitcast(I32), picked[:].bitcast(I32))
-            for r in range(1, 4):
-                nc.scalar.dma_start(
-                    placed[row + r : P : 32, :].bitcast(I32), picked[row + SPREAD * r : P : 32, :].bitcast(I32)
-                )
-            return placed
-
         warm = pool.tile([P, 2], F32, name="warm")
         nc.gpsimd.memset(warm[:, 0:1], 0.0)
         nc.scalar.activation(warm[:, 1:2], warm[:, 0:1], mybir.ActivationFunctionType.Silu)
-        nc.vector.memset(k_plane[:].bitcast(I32), 0)
+        k_bytes = pool.tile([P, N], U8, name="k_bytes", align_bytes=64)
+        c_bytes = pool.tile([P, N], U8, name="c_bytes", align_bytes=64)
         nc.vector.memset(c_plane[:].bitcast(I32), 0)
+        nc.vector.memset(k_plane[:TOP, :].bitcast(I32), 0)
+        nc.vector.memset(k_bytes[:].bitcast(I32), 0)
+        nc.sync.dma_start(k_plane[TOP:, :].bitcast(I32), k_scales[0].bitcast(I32))
         nc.sync.dma_start(offsets[:], offs)
         nc.sync.dma_start(q_raw[:], qT[0].rearrange("(p j) q -> p j q", j=PACK))
-        load_rows(k_plane, 0, k_scales)
-        load_rows(c_plane, C_ROW, c_scales)
+        for r in range(2):
+            nc.sync.dma_start(c_plane[C_ROW + r : P : 16, :].bitcast(I32), c_scales[0, r:16:2, :].bitcast(I32))
         nc.sync.dma_start(k_table[:], words(k_words))
         nc.sync.dma_start(c_table[:, :REACH], words(c_words)[:, :REACH])
         nc.sync.dma_start(c_table[:, REACH:], words(c_words)[:, REACH:])
@@ -68,8 +58,17 @@ def tile_attend_neu_swiglu_srt_kernel(tc, qT, k_words, k_scales, c_words, c_scal
         q_codes = pool.tile([P, NQ], U32, name="q_codes", align_bytes=64)
         q_plane = pool.tile([P, NQ], U8, name="q_plane", align_bytes=64)
         nc.scalar.copy(out=q_grouped[:], in_=q_raw[:].rearrange("p j q -> p q j"))
-        k_bytes = pick_rows("k", k_plane, 0)
-        c_bytes = pick_rows("c", c_plane, C_ROW)
+        k_listed = pool.tile([P, N], U8, name="k_listed", align_bytes=64)
+        nc.vector.tensor_copy(k_listed[:], k_plane[:].indirect(offsets[:]))
+        for r in range(4):
+            nc.scalar.dma_start(k_bytes[r:P:32, :].bitcast(I32), k_listed[TOP + r : P : 4, :].bitcast(I32))
+        c_listed = pool.tile([P, N], U8, name="c_listed", align_bytes=64)
+        nc.vector.tensor_copy(c_listed[:], c_plane[:].indirect(offsets[:]))
+        nc.vector.tensor_copy(c_bytes[:].bitcast(I32), c_listed[:].bitcast(I32))
+        for r in range(2):
+            nc.scalar.dma_start(
+                c_bytes[C_ROW + 2 + r : P : 32, :].bitcast(I32), c_listed[C_ROW + 16 + r : P : 32, :].bitcast(I32)
+            )
         nc.vector.quantize_mx(
             out=q_codes[:].bitcast(FP8X4), scales=q_plane[:], in_=q_grouped[:].rearrange("p q j -> p (q j)")
         )

@@ -37,17 +37,17 @@ def tile_attend_neu_swiglu_srt_kernel(tc, qT, k_words, k_scales, c_words, c_scal
         def words(dram):
             return dram[0].rearrange("p t r -> p (t r)").bitcast(I32)
 
-        warm = pool.tile([P, 2], F32, name="warm")
-        nc.gpsimd.memset(warm[:, 0:1], 0.0)
-        nc.scalar.activation(warm[:, 1:2], warm[:, 0:1], mybir.ActivationFunctionType.Silu)
         k_bytes = pool.tile([P, N], U8, name="k_bytes", align_bytes=64)
         c_bytes = pool.tile([P, N], U8, name="c_bytes", align_bytes=64)
         nc.vector.memset(c_plane[:].bitcast(I32), 0)
         nc.vector.memset(k_plane[:TOP, :].bitcast(I32), 0)
         nc.vector.memset(k_bytes[:].bitcast(I32), 0)
-        nc.sync.dma_start(k_plane[TOP:, :].bitcast(I32), k_scales[0].bitcast(I32))
+        nc.scalar.dma_start(k_plane[TOP:, :].bitcast(I32), k_scales[0].bitcast(I32))
         nc.sync.dma_start(offsets[:], offs)
         nc.sync.dma_start(q_raw[:], qT[0].rearrange("(p j) q -> p j q", j=PACK))
+        warm = pool.tile([P, 2], F32, name="warm")
+        nc.vector.memset(warm[:, 0:1], 0.0)
+        nc.scalar.activation(warm[:, 1:2], warm[:, 0:1], mybir.ActivationFunctionType.Silu)
         for r in range(2):
             nc.sync.dma_start(c_plane[C_ROW + r : P : 16, :].bitcast(I32), c_scales[0, r:16:2, :].bitcast(I32))
         nc.sync.dma_start(k_table[:], words(k_words))

@@ -16,6 +16,7 @@ FP8X4 = mybir.dt.float8_e4m3fn_x4
 P = 128
 PACK = 4
 HALF = N // 2
+QUARTER = N // 4
 C_ROW = 4
 TOP = 112
 REACH = T - HALF
@@ -97,9 +98,27 @@ def tile_attend_neu_swiglu_srt_kernel(tc, qT, k_words, k_scales, c_words, c_scal
             gates.append(gate)
 
         c_picked = pool.tile([P, N], U32, name="c_picked", tag="c_slot", align_bytes=64)
-        layers = [product("c", c_table, c_picked, c_bytes, C_ROW, h) for h in range(2)]
-        for h in range(2):
-            result = pool.tile([NQ, HALF], F32, name="result%d" % h)
-            nc.vector.tensor_tensor(result[:], layers[h][:], gates[h][:], mybir.AluOpType.mult)
-            queue = nc.sync if h == 0 else nc.scalar
-            queue.dma_start(out[0, :, h * HALF : (h + 1) * HALF], result[:])
+        layer = product("c", c_table, c_picked, c_bytes, C_ROW, 0)
+        nc.vector.tensor_copy(c_picked[:, HALF:], c_table[:].bitcast(U32).indirect(offsets[:, HALF // 16 :]))
+        quarters = []
+        for j in range(2):
+            cols = slice(HALF + j * QUARTER, HALF + (j + 1) * QUARTER)
+            acc = psum.tile([NQ, QUARTER], F32, name="c_quarter%d" % j)
+            nc.tensor.matmul_mx(
+                out=acc[:],
+                lhsT=q_codes[:].bitcast(FP8X4),
+                lhsT_scale=q_plane[:],
+                rhs=c_picked[:, cols].bitcast(FP8X4),
+                rhs_scale=c_bytes[C_ROW:P, cols],
+                start=True,
+                stop=True,
+            )
+            quarters.append(acc)
+        first = pool.tile([NQ, HALF], F32, name="first")
+        nc.vector.tensor_tensor(first[:], layer[:], gates[0][:], mybir.AluOpType.mult)
+        nc.sync.dma_start(out[0, :, :HALF], first[:])
+        second = pool.tile([NQ, HALF], F32, name="second")
+        for j in range(2):
+            cols = slice(j * QUARTER, (j + 1) * QUARTER)
+            nc.vector.tensor_tensor(second[:, cols], quarters[j][:], gates[1][:, cols], mybir.AluOpType.mult)
+        nc.scalar.dma_start(out[0, :, HALF:], second[:])

@@ -28,18 +28,18 @@ def tile_attend_neu_swiglu_srt_kernel(tc, qT, k_words, k_scales, c_words, c_scal
         pool = ctx.enter_context(tc.tile_pool(name="sbuf", bufs=1))
         psum = ctx.enter_context(tc.psum_pool(name="psum", bufs=1))
 
-        offsets = pool.tile([P, N // 16], U16, name="offsets")
-        k_table = pool.tile([P, T], I32, name="k_table", align_bytes=64)
-        c_table = pool.tile([P, T], I32, name="c_table", align_bytes=64)
-        k_plane = pool.tile([P, T], U8, name="k_plane", tag="k_slot", align_bytes=64)
-        c_plane = pool.tile([P, T], U8, name="c_plane", tag="c_slot", align_bytes=64)
-        q_raw = pool.tile([P, PACK, NQ], F32, name="q_raw", align_bytes=64)
+        offsets = pool.tile([P, N // 16], U16, name="offsets", align_bytes=256)
+        k_table = pool.tile([P, T], I32, name="k_table", align_bytes=256)
+        c_table = pool.tile([P, T], I32, name="c_table", align_bytes=256)
+        k_plane = pool.tile([P, T], U8, name="k_plane", tag="k_slot", align_bytes=256)
+        c_plane = pool.tile([P, T], U8, name="c_plane", tag="c_slot", align_bytes=256)
+        q_raw = pool.tile([P, PACK, NQ], F32, name="q_raw", align_bytes=256)
 
         def words(dram):
             return dram[0].rearrange("p t r -> p (t r)").bitcast(I32)
 
-        k_bytes = pool.tile([P, N], U8, name="k_bytes", align_bytes=64)
-        c_bytes = pool.tile([P, N], U8, name="c_bytes", align_bytes=64)
+        k_bytes = pool.tile([P, N], U8, name="k_bytes", align_bytes=256)
+        c_bytes = pool.tile([P, N], U8, name="c_bytes", align_bytes=256)
         nc.vector.memset(c_plane[:].bitcast(I32), 0)
         nc.vector.memset(k_plane[:TOP, :].bitcast(I32), 0)
         nc.vector.memset(k_bytes[:].bitcast(I32), 0)
@@ -55,15 +55,15 @@ def tile_attend_neu_swiglu_srt_kernel(tc, qT, k_words, k_scales, c_words, c_scal
         nc.sync.dma_start(c_table[:, :REACH], words(c_words)[:, :REACH])
         nc.sync.dma_start(c_table[:, REACH:], words(c_words)[:, REACH:])
 
-        q_grouped = pool.tile([P, NQ, PACK], BF16, name="q_grouped", align_bytes=64)
-        q_codes = pool.tile([P, NQ], U32, name="q_codes", align_bytes=64)
-        q_plane = pool.tile([P, NQ], U8, name="q_plane", align_bytes=64)
+        q_grouped = pool.tile([P, NQ, PACK], BF16, name="q_grouped", align_bytes=256)
+        q_codes = pool.tile([P, NQ], U32, name="q_codes", align_bytes=256)
+        q_plane = pool.tile([P, NQ], U8, name="q_plane", align_bytes=256)
         nc.scalar.copy(out=q_grouped[:], in_=q_raw[:].rearrange("p j q -> p q j"))
-        k_listed = pool.tile([P, N], U8, name="k_listed", align_bytes=64)
+        k_listed = pool.tile([P, N], U8, name="k_listed", align_bytes=256)
         nc.vector.tensor_copy(k_listed[:], k_plane[:].indirect(offsets[:]))
         for r in range(4):
             nc.scalar.dma_start(k_bytes[r:P:32, :].bitcast(I32), k_listed[TOP + r : P : 4, :].bitcast(I32))
-        c_listed = pool.tile([P, N], U8, name="c_listed", align_bytes=64)
+        c_listed = pool.tile([P, N], U8, name="c_listed", align_bytes=256)
         nc.vector.tensor_copy(c_listed[:], c_plane[:].indirect(offsets[:]))
         nc.vector.tensor_copy(c_bytes[:].bitcast(I32), c_listed[:].bitcast(I32))
         for r in range(2):
@@ -90,14 +90,14 @@ def tile_attend_neu_swiglu_srt_kernel(tc, qT, k_words, k_scales, c_words, c_scal
             return acc
 
         gates = []
-        k_picked = pool.tile([P, N], U32, name="k_picked", tag="k_slot", align_bytes=64)
+        k_picked = pool.tile([P, N], U32, name="k_picked", tag="k_slot", align_bytes=256)
         for h in range(2):
             acc = product("k", k_table, k_picked, k_bytes, 0, h)
-            gate = pool.tile([NQ, HALF], F32, name="gate%d" % h)
+            gate = pool.tile([NQ, HALF], F32, name="gate%d" % h, align_bytes=256)
             nc.scalar.activation(gate[:], acc[:], mybir.ActivationFunctionType.Silu)
             gates.append(gate)
 
-        c_picked = pool.tile([P, N], U32, name="c_picked", tag="c_slot", align_bytes=64)
+        c_picked = pool.tile([P, N], U32, name="c_picked", tag="c_slot", align_bytes=256)
         layer = product("c", c_table, c_picked, c_bytes, C_ROW, 0)
         nc.vector.tensor_copy(c_picked[:, HALF:], c_table[:].bitcast(U32).indirect(offsets[:, HALF // 16 :]))
         quarters = []
@@ -114,10 +114,10 @@ def tile_attend_neu_swiglu_srt_kernel(tc, qT, k_words, k_scales, c_words, c_scal
                 stop=True,
             )
             quarters.append(acc)
-        first = pool.tile([NQ, HALF], F32, name="first")
+        first = pool.tile([NQ, HALF], F32, name="first", align_bytes=256)
         nc.vector.tensor_tensor(first[:], layer[:], gates[0][:], mybir.AluOpType.mult)
         nc.sync.dma_start(out[0, :, :HALF], first[:])
-        second = pool.tile([NQ, HALF], F32, name="second")
+        second = pool.tile([NQ, HALF], F32, name="second", align_bytes=256)
         for j in range(2):
             cols = slice(j * QUARTER, (j + 1) * QUARTER)
             nc.vector.tensor_tensor(second[:, cols], quarters[j][:], gates[1][:, cols], mybir.AluOpType.mult)

@@ -44,8 +44,8 @@ def tile_attend_neu_swiglu_srt_kernel(tc, qT, k_words, k_scales, c_words, c_scal
         nc.vector.memset(k_plane[:TOP, :].bitcast(I32), 0)
         nc.vector.memset(k_bytes[:].bitcast(I32), 0)
         nc.scalar.dma_start(k_plane[TOP:, :].bitcast(I32), k_scales[0].bitcast(I32))
-        nc.sync.dma_start(offsets[:], offs)
         nc.sync.dma_start(q_raw[:], qT[0].rearrange("(p j) q -> p j q", j=PACK))
+        nc.sync.dma_start(offsets[:], offs)
         warm = pool.tile([P, 2], F32, name="warm")
         nc.vector.memset(warm[:, 0:1], 0.0)
         nc.scalar.activation(warm[:, 1:2], warm[:, 0:1], mybir.ActivationFunctionType.Silu)

@@ -17,7 +17,7 @@ P = 128
 PACK = 4
 HALF = N // 2
 QUARTER = N // 4
-C_ROW = 4
+C_ROW = 8
 TOP = 112
 REACH = T - HALF
 
@@ -40,17 +40,19 @@ def tile_attend_neu_swiglu_srt_kernel(tc, qT, k_words, k_scales, c_words, c_scal
 
         k_bytes = pool.tile([P, N], U8, name="k_bytes", align_bytes=256)
         c_bytes = pool.tile([P, N], U8, name="c_bytes", align_bytes=256)
+        warm = pool.tile([P, 2], F32, name="warm")
+        nc.gpsimd.memset(warm[:, 0:1], 0.0)
         nc.vector.memset(c_plane[:].bitcast(I32), 0)
         nc.vector.memset(k_plane[:TOP, :].bitcast(I32), 0)
         nc.vector.memset(k_bytes[:].bitcast(I32), 0)
         nc.scalar.dma_start(k_plane[TOP:, :].bitcast(I32), k_scales[0].bitcast(I32))
         nc.sync.dma_start(q_raw[:], qT[0].rearrange("(p j) q -> p j q", j=PACK))
         nc.sync.dma_start(offsets[:], offs)
-        warm = pool.tile([P, 2], F32, name="warm")
-        nc.vector.memset(warm[:, 0:1], 0.0)
         nc.scalar.activation(warm[:, 1:2], warm[:, 0:1], mybir.ActivationFunctionType.Silu)
         for r in range(2):
-            nc.sync.dma_start(c_plane[C_ROW + r : P : 16, :].bitcast(I32), c_scales[0, r:16:2, :].bitcast(I32))
+            (nc.sync, nc.scalar)[r].dma_start(
+                c_plane[64 * r + C_ROW : 64 * r + C_ROW + 8, :].bitcast(I32), c_scales[0, 8 * r : 8 * r + 8, :].bitcast(I32)
+            )
         nc.sync.dma_start(k_table[:], words(k_words))
         nc.sync.dma_start(c_table[:, :REACH], words(c_words)[:, :REACH])
         nc.sync.dma_start(c_table[:, REACH:], words(c_words)[:, REACH:])
@@ -68,7 +70,8 @@ def tile_attend_neu_swiglu_srt_kernel(tc, qT, k_words, k_scales, c_words, c_scal
         nc.vector.tensor_copy(c_bytes[:].bitcast(I32), c_listed[:].bitcast(I32))
         for r in range(2):
             nc.scalar.dma_start(
-                c_bytes[C_ROW + 2 + r : P : 32, :].bitcast(I32), c_listed[C_ROW + 16 + r : P : 32, :].bitcast(I32)
+                c_bytes[64 * r + 32 + C_ROW : 64 * r + 36 + C_ROW, :].bitcast(I32),
+                c_listed[64 * r + C_ROW + 4 : 64 * r + C_ROW + 8, :].bitcast(I32),
             )
         nc.vector.quantize_mx(
             out=q_codes[:].bitcast(FP8X4), scales=q_plane[:], in_=q_grouped[:].rearrange("p q j -> p (q j)")

@@ -92,36 +92,30 @@ def tile_attend_neu_swiglu_srt_kernel(tc, qT, k_words, k_scales, c_words, c_scal
             )
             return acc
 
-        gates = []
+        gate = pool.tile([NQ, N], F32, name="gate", align_bytes=256)
         k_picked = pool.tile([P, N], U32, name="k_picked", tag="k_slot", align_bytes=256)
         for h in range(2):
             acc = product("k", k_table, k_picked, k_bytes, 0, h)
-            gate = pool.tile([NQ, HALF], F32, name="gate%d" % h, align_bytes=256)
-            nc.scalar.activation(gate[:], acc[:], mybir.ActivationFunctionType.Silu)
-            gates.append(gate)
+            nc.scalar.activation(gate[:, h * HALF : (h + 1) * HALF], acc[:], mybir.ActivationFunctionType.Silu)
 
         c_picked = pool.tile([P, N], U32, name="c_picked", tag="c_slot", align_bytes=256)
-        layer = product("c", c_table, c_picked, c_bytes, C_ROW, 0)
-        nc.vector.tensor_copy(c_picked[:, HALF:], c_table[:].bitcast(U32).indirect(offsets[:, HALF // 16 :]))
-        quarters = []
-        for j in range(2):
-            cols = slice(HALF + j * QUARTER, HALF + (j + 1) * QUARTER)
-            acc = psum.tile([NQ, QUARTER], F32, name="c_quarter%d" % j)
+        pieces = ((0, HALF, REACH), (HALF, HALF + QUARTER, T), (HALF + QUARTER, N, T))
+        layers = []
+        for a, b, reach in pieces:
+            nc.vector.tensor_copy(c_picked[:, a:b], c_table[:, :reach].bitcast(U32).indirect(offsets[:, a // 16 : b // 16]))
+            acc = psum.tile([NQ, b - a], F32, name="c_acc%d" % a)
             nc.tensor.matmul_mx(
                 out=acc[:],
                 lhsT=q_codes[:].bitcast(FP8X4),
                 lhsT_scale=q_plane[:],
-                rhs=c_picked[:, cols].bitcast(FP8X4),
-                rhs_scale=c_bytes[C_ROW:P, cols],
+                rhs=c_picked[:, a:b].bitcast(FP8X4),
+                rhs_scale=c_bytes[C_ROW:P, a:b],
                 start=True,
                 stop=True,
             )
-            quarters.append(acc)
-        first = pool.tile([NQ, HALF], F32, name="first", align_bytes=256)
-        nc.vector.tensor_tensor(first[:], layer[:], gates[0][:], mybir.AluOpType.mult)
-        nc.sync.dma_start(out[0, :, :HALF], first[:])
-        second = pool.tile([NQ, HALF], F32, name="second", align_bytes=256)
-        for j in range(2):
-            cols = slice(j * QUARTER, (j + 1) * QUARTER)
-            nc.vector.tensor_tensor(second[:, cols], quarters[j][:], gates[1][:, cols], mybir.AluOpType.mult)
-        nc.scalar.dma_start(out[0, :, HALF:], second[:])
+            layers.append(acc)
+        result = pool.tile([NQ, N], F32, name="result", align_bytes=256)
+        for (a, b, reach), acc in zip(pieces, layers):
+            nc.vector.tensor_tensor(result[:, a:b], acc[:], gate[:, a:b], mybir.AluOpType.mult)
+        nc.sync.dma_start(out[0, :, : N - QUARTER], result[:, : N - QUARTER])
+        nc.scalar.dma_start(out[0, :, N - QUARTER :], result[:, N - QUARTER :])

@@ -117,5 +117,5 @@ def tile_attend_neu_swiglu_srt_kernel(tc, qT, k_words, k_scales, c_words, c_scal
         result = pool.tile([NQ, N], F32, name="result", align_bytes=256)
         for (a, b, reach), acc in zip(pieces, layers):
             nc.vector.tensor_tensor(result[:, a:b], acc[:], gate[:, a:b], mybir.AluOpType.mult)
-        nc.sync.dma_start(out[0, :, : N - QUARTER], result[:, : N - QUARTER])
-        nc.scalar.dma_start(out[0, :, N - QUARTER :], result[:, N - QUARTER :])
+        nc.sync.dma_start(out[0, :, :HALF], result[:, :HALF])
+        nc.scalar.dma_start(out[0, :, HALF:], result[:, HALF:])

@@ -117,5 +117,5 @@ def tile_attend_neu_swiglu_srt_kernel(tc, qT, k_words, k_scales, c_words, c_scal
         result = pool.tile([NQ, N], F32, name="result", align_bytes=256)
         for (a, b, reach), acc in zip(pieces, layers):
             nc.vector.tensor_tensor(result[:, a:b], acc[:], gate[:, a:b], mybir.AluOpType.mult)
-        nc.sync.dma_start(out[0, :, :HALF], result[:, :HALF])
-        nc.scalar.dma_start(out[0, :, HALF:], result[:, HALF:])
+        for (a, b, reach), queue in zip(pieces, (nc.scalar, nc.scalar, nc.sync)):
+            queue.dma_start(out[0, :, a:b], result[:, a:b])

@@ -99,23 +99,25 @@ def tile_attend_neu_swiglu_srt_kernel(tc, qT, k_words, k_scales, c_words, c_scal
             nc.scalar.activation(gate[:, h * HALF : (h + 1) * HALF], acc[:], mybir.ActivationFunctionType.Silu)
 
         c_picked = pool.tile([P, N], U32, name="c_picked", tag="c_slot", align_bytes=256)
-        pieces = ((0, HALF, REACH), (HALF, HALF + QUARTER, T), (HALF + QUARTER, N, T))
+        gathers = ((0, HALF, REACH), (HALF, HALF + QUARTER, T), (HALF + QUARTER, N, T))
         layers = []
-        for a, b, reach in pieces:
+        for a, b, reach in gathers:
             nc.vector.tensor_copy(c_picked[:, a:b], c_table[:, :reach].bitcast(U32).indirect(offsets[:, a // 16 : b // 16]))
-            acc = psum.tile([NQ, b - a], F32, name="c_acc%d" % a)
-            nc.tensor.matmul_mx(
-                out=acc[:],
-                lhsT=q_codes[:].bitcast(FP8X4),
-                lhsT_scale=q_plane[:],
-                rhs=c_picked[:, a:b].bitcast(FP8X4),
-                rhs_scale=c_bytes[C_ROW:P, a:b],
-                start=True,
-                stop=True,
-            )
-            layers.append(acc)
+            for start in range(a, b, QUARTER):
+                cols = slice(start, start + QUARTER)
+                acc = psum.tile([NQ, QUARTER], F32, name="c_acc%d" % start)
+                nc.tensor.matmul_mx(
+                    out=acc[:],
+                    lhsT=q_codes[:].bitcast(FP8X4),
+                    lhsT_scale=q_plane[:],
+                    rhs=c_picked[:, cols].bitcast(FP8X4),
+                    rhs_scale=c_bytes[C_ROW:P, cols],
+                    start=True,
+                    stop=True,
+                )
+                layers.append((cols, acc))
         result = pool.tile([NQ, N], F32, name="result", align_bytes=256)
-        for (a, b, reach), acc in zip(pieces, layers):
-            nc.vector.tensor_tensor(result[:, a:b], acc[:], gate[:, a:b], mybir.AluOpType.mult)
-        for (a, b, reach), queue in zip(pieces, (nc.scalar, nc.scalar, nc.sync)):
+        for cols, acc in layers:
+            nc.vector.tensor_tensor(result[:, cols], acc[:], gate[:, cols], mybir.AluOpType.mult)
+        for (a, b, reach), queue in zip(gathers, (nc.scalar, nc.scalar, nc.sync)):
             queue.dma_start(out[0, :, a:b], result[:, a:b])

@@ -117,7 +117,10 @@ def tile_attend_neu_swiglu_srt_kernel(tc, qT, k_words, k_scales, c_words, c_scal
                 )
                 layers.append((cols, acc))
         result = pool.tile([NQ, N], F32, name="result", align_bytes=256)
+        cut = QUARTER + QUARTER // 2
         for cols, acc in layers:
-            nc.vector.tensor_tensor(result[:, cols], acc[:], gate[:, cols], mybir.AluOpType.mult)
-        for (a, b, reach), queue in zip(gathers, (nc.scalar, nc.scalar, nc.sync)):
+            edges = sorted({cols.start, cols.stop} | ({cut} if cols.start < cut < cols.stop else set()))
+            for a, b in zip(edges, edges[1:]):
+                nc.vector.tensor_tensor(result[:, a:b], acc[:, a - cols.start : b - cols.start], gate[:, a:b], mybir.AluOpType.mult)
+        for a, b, queue in ((0, cut, nc.scalar), (cut, N - QUARTER, nc.scalar), (N - QUARTER, N, nc.sync)):
             queue.dma_start(out[0, :, a:b], result[:, a:b])

@@ -57,7 +57,7 @@ def tile_attend_neu_swiglu_srt_kernel(tc, qT, k_words, k_scales, c_words, c_scal
         nc.sync.dma_start(c_table[:, :REACH], words(c_words)[:, :REACH])
         nc.sync.dma_start(c_table[:, REACH:], words(c_words)[:, REACH:])
 
-        q_grouped = pool.tile([P, NQ, PACK], BF16, name="q_grouped", align_bytes=256)
+        q_grouped = pool.tile([P, NQ, PACK], BF16, name="q_grouped", tag="q_slot", align_bytes=256)
         q_codes = pool.tile([P, NQ], U32, name="q_codes", align_bytes=256)
         q_plane = pool.tile([P, NQ], U8, name="q_plane", align_bytes=256)
         nc.scalar.copy(out=q_grouped[:], in_=q_raw[:].rearrange("p j q -> p q j"))
@@ -65,7 +65,10 @@ def tile_attend_neu_swiglu_srt_kernel(tc, qT, k_words, k_scales, c_words, c_scal
         nc.vector.tensor_copy(k_listed[:], k_plane[:].indirect(offsets[:]))
         for r in range(4):
             nc.scalar.dma_start(k_bytes[r:P:32, :].bitcast(I32), k_listed[TOP + r : P : 4, :].bitcast(I32))
-        c_listed = pool.tile([P, N], U8, name="c_listed", align_bytes=256)
+        nc.vector.quantize_mx(
+            out=q_codes[:].bitcast(FP8X4), scales=q_plane[:], in_=q_grouped[:].rearrange("p q j -> p (q j)")
+        )
+        c_listed = pool.tile([P, N], U8, name="c_listed", tag="q_slot", align_bytes=256)
         nc.vector.tensor_copy(c_listed[:], c_plane[:].indirect(offsets[:]))
         nc.vector.tensor_copy(c_bytes[:].bitcast(I32), c_listed[:].bitcast(I32))
         for r in range(2):
@@ -73,9 +76,6 @@ def tile_attend_neu_swiglu_srt_kernel(tc, qT, k_words, k_scales, c_words, c_scal
                 c_bytes[64 * r + 32 + C_ROW : 64 * r + 36 + C_ROW, :].bitcast(I32),
                 c_listed[64 * r + C_ROW + 4 : 64 * r + C_ROW + 8, :].bitcast(I32),
             )
-        nc.vector.quantize_mx(
-            out=q_codes[:].bitcast(FP8X4), scales=q_plane[:], in_=q_grouped[:].rearrange("p q j -> p (q j)")
-        )
 
         def product(name, table, picked, picked_bytes, row, h):
             cols = slice(h * HALF, (h + 1) * HALF)

@@ -55,7 +55,6 @@ def tile_attend_neu_swiglu_srt_kernel(tc, qT, k_words, k_scales, c_words, c_scal
             )
         nc.sync.dma_start(k_table[:], words(k_words))
         nc.sync.dma_start(c_table[:, :REACH], words(c_words)[:, :REACH])
-        nc.sync.dma_start(c_table[:, REACH:], words(c_words)[:, REACH:])
 
         q_grouped = pool.tile([P, NQ, PACK], BF16, name="q_grouped", tag="q_slot", align_bytes=256)
         q_codes = pool.tile([P, NQ], U32, name="q_codes", align_bytes=256)
@@ -64,7 +63,8 @@ def tile_attend_neu_swiglu_srt_kernel(tc, qT, k_words, k_scales, c_words, c_scal
         k_listed = pool.tile([P, N], U8, name="k_listed", align_bytes=256)
         nc.vector.tensor_copy(k_listed[:], k_plane[:].indirect(offsets[:]))
         for r in range(4):
-            nc.scalar.dma_start(k_bytes[r:P:32, :].bitcast(I32), k_listed[TOP + r : P : 4, :].bitcast(I32))
+            nc.sync.dma_start(k_bytes[r:P:32, :].bitcast(I32), k_listed[TOP + r : P : 4, :].bitcast(I32))
+        nc.sync.dma_start(c_table[:, REACH:], words(c_words)[:, REACH:])
         nc.vector.quantize_mx(
             out=q_codes[:].bitcast(FP8X4), scales=q_plane[:], in_=q_grouped[:].rearrange("p q j -> p (q j)")
         )
@@ -72,7 +72,7 @@ def tile_attend_neu_swiglu_srt_kernel(tc, qT, k_words, k_scales, c_words, c_scal
         nc.vector.tensor_copy(c_listed[:], c_plane[:].indirect(offsets[:]))
         nc.vector.tensor_copy(c_bytes[:].bitcast(I32), c_listed[:].bitcast(I32))
         for r in range(2):
-            nc.scalar.dma_start(
+            nc.sync.dma_start(
                 c_bytes[64 * r + 32 + C_ROW : 64 * r + 36 + C_ROW, :].bitcast(I32),
                 c_listed[64 * r + C_ROW + 4 : 64 * r + C_ROW + 8, :].bitcast(I32),
             )

@@ -17,7 +17,7 @@ P = 128
 PACK = 4
 HALF = N // 2
 QUARTER = N // 4
-C_ROW = 8
+K_ROW = 8
 TOP = 112
 REACH = T - HALF
 
@@ -42,40 +42,40 @@ def tile_attend_neu_swiglu_srt_kernel(tc, qT, k_words, k_scales, c_words, c_scal
         c_bytes = pool.tile([P, N], U8, name="c_bytes", align_bytes=256)
         warm = pool.tile([P, 2], F32, name="warm")
         nc.gpsimd.memset(warm[:, 0:1], 0.0)
-        nc.vector.memset(c_plane[:].bitcast(I32), 0)
-        nc.vector.memset(k_plane[:TOP, :].bitcast(I32), 0)
-        nc.vector.memset(k_bytes[:].bitcast(I32), 0)
-        nc.scalar.dma_start(k_plane[TOP:, :].bitcast(I32), k_scales[0].bitcast(I32))
-        nc.sync.dma_start(q_raw[:], qT[0].rearrange("(p j) q -> p j q", j=PACK))
+        nc.vector.memset(k_plane[:].bitcast(I32), 0)
+        nc.vector.memset(c_plane[:TOP, :].bitcast(I32), 0)
+        nc.vector.memset(c_bytes[:].bitcast(I32), 0)
+        nc.scalar.dma_start(c_plane[TOP:, :].bitcast(I32), c_scales[0].bitcast(I32))
         nc.sync.dma_start(offsets[:], offs)
+        nc.sync.dma_start(q_raw[:], qT[0].rearrange("(p j) q -> p j q", j=PACK))
         nc.scalar.activation(warm[:, 1:2], warm[:, 0:1], mybir.ActivationFunctionType.Silu)
         for r in range(2):
             (nc.sync, nc.scalar)[r].dma_start(
-                c_plane[64 * r + C_ROW : 64 * r + C_ROW + 8, :].bitcast(I32), c_scales[0, 8 * r : 8 * r + 8, :].bitcast(I32)
+                k_plane[64 * r + K_ROW : 64 * r + K_ROW + 8, :].bitcast(I32), k_scales[0, 8 * r : 8 * r + 8, :].bitcast(I32)
             )
         nc.sync.dma_start(k_table[:], words(k_words))
         nc.sync.dma_start(c_table[:, :REACH], words(c_words)[:, :REACH])
 
-        q_grouped = pool.tile([P, NQ, PACK], BF16, name="q_grouped", tag="q_slot", align_bytes=256)
-        q_codes = pool.tile([P, NQ], U32, name="q_codes", align_bytes=256)
+        q_grouped = pool.tile([P, NQ, PACK], BF16, name="q_grouped", align_bytes=256)
+        q_codes = pool.tile([P, NQ], U32, name="q_codes", tag="k_slot", align_bytes=256)
         q_plane = pool.tile([P, NQ], U8, name="q_plane", align_bytes=256)
         nc.scalar.copy(out=q_grouped[:], in_=q_raw[:].rearrange("p j q -> p q j"))
+        c_listed = pool.tile([P, N], U8, name="c_listed", align_bytes=256)
+        nc.vector.tensor_copy(c_listed[:], c_plane[:].indirect(offsets[:]))
         k_listed = pool.tile([P, N], U8, name="k_listed", align_bytes=256)
         nc.vector.tensor_copy(k_listed[:], k_plane[:].indirect(offsets[:]))
-        for r in range(4):
-            nc.sync.dma_start(k_bytes[r:P:32, :].bitcast(I32), k_listed[TOP + r : P : 4, :].bitcast(I32))
+        nc.vector.tensor_copy(k_bytes[:].bitcast(I32), k_listed[:].bitcast(I32))
+        for r in range(2):
+            nc.sync.dma_start(
+                k_bytes[64 * r + 32 + K_ROW : 64 * r + 36 + K_ROW, :].bitcast(I32),
+                k_listed[64 * r + K_ROW + 4 : 64 * r + K_ROW + 8, :].bitcast(I32),
+            )
         nc.sync.dma_start(c_table[:, REACH:], words(c_words)[:, REACH:])
+        for r in range(4):
+            nc.sync.dma_start(c_bytes[r:P:32, :].bitcast(I32), c_listed[TOP + r : P : 4, :].bitcast(I32))
         nc.vector.quantize_mx(
             out=q_codes[:].bitcast(FP8X4), scales=q_plane[:], in_=q_grouped[:].rearrange("p q j -> p (q j)")
         )
-        c_listed = pool.tile([P, N], U8, name="c_listed", tag="q_slot", align_bytes=256)
-        nc.vector.tensor_copy(c_listed[:], c_plane[:].indirect(offsets[:]))
-        nc.vector.tensor_copy(c_bytes[:].bitcast(I32), c_listed[:].bitcast(I32))
-        for r in range(2):
-            nc.sync.dma_start(
-                c_bytes[64 * r + 32 + C_ROW : 64 * r + 36 + C_ROW, :].bitcast(I32),
-                c_listed[64 * r + C_ROW + 4 : 64 * r + C_ROW + 8, :].bitcast(I32),
-            )
 
         def product(name, table, picked, picked_bytes, row, h):
             cols = slice(h * HALF, (h + 1) * HALF)
@@ -93,12 +93,12 @@ def tile_attend_neu_swiglu_srt_kernel(tc, qT, k_words, k_scales, c_words, c_scal
             return acc
 
         gate = pool.tile([NQ, N], F32, name="gate", align_bytes=256)
-        k_picked = pool.tile([P, N], U32, name="k_picked", tag="k_slot", align_bytes=256)
+        k_picked = pool.tile([P, N], U32, name="k_picked", tag="c_slot", align_bytes=256)
         for h in range(2):
-            acc = product("k", k_table, k_picked, k_bytes, 0, h)
+            acc = product("k", k_table, k_picked, k_bytes, K_ROW, h)
             nc.scalar.activation(gate[:, h * HALF : (h + 1) * HALF], acc[:], mybir.ActivationFunctionType.Silu)
 
-        c_picked = pool.tile([P, N], U32, name="c_picked", tag="c_slot", align_bytes=256)
+        c_picked = pool.tile([P, N], U32, name="c_picked", align_bytes=256)
         gathers = ((0, HALF, REACH), (HALF, HALF + QUARTER, T), (HALF + QUARTER, N, T))
         layers = []
         for a, b, reach in gathers:
@@ -111,7 +111,7 @@ def tile_attend_neu_swiglu_srt_kernel(tc, qT, k_words, k_scales, c_words, c_scal
                     lhsT=q_codes[:].bitcast(FP8X4),
                     lhsT_scale=q_plane[:],
                     rhs=c_picked[:, cols].bitcast(FP8X4),
-                    rhs_scale=c_bytes[C_ROW:P, cols],
+                    rhs_scale=c_bytes[:, cols],
                     start=True,
                     stop=True,
                 )

from contextlib import ExitStack

import concourse.mybir as mybir

T, N, D, NQ = 2048, 512, 512, 128
FLOPS = 2 * 2 * D * NQ * N

F32 = mybir.dt.float32
BF16 = mybir.dt.bfloat16
I32 = mybir.dt.int32
U32 = mybir.dt.uint32
U16 = mybir.dt.uint16
U8 = mybir.dt.uint8
FP8X4 = mybir.dt.float8_e4m3fn_x4

P = 128
PACK = 4
HALF = N // 2
QUARTER = N // 4
K_ROW = 8
TOP = 112
REACH = T - HALF


def tile_attend_neu_swiglu_srt_kernel(tc, qT, k_words, k_scales, c_words, c_scales, offs, out):
    nc = tc.nc
    with ExitStack() as ctx:
        pool = ctx.enter_context(tc.tile_pool(name="sbuf", bufs=1))
        psum = ctx.enter_context(tc.psum_pool(name="psum", bufs=1))

        offsets = pool.tile([P, N // 16], U16, name="offsets", align_bytes=256)
        k_table = pool.tile([P, T], I32, name="k_table", align_bytes=256)
        c_table = pool.tile([P, T], I32, name="c_table", align_bytes=256)
        k_plane = pool.tile([P, T], U8, name="k_plane", tag="k_slot", align_bytes=256)
        c_plane = pool.tile([P, T], U8, name="c_plane", tag="c_slot", align_bytes=256)
        q_raw = pool.tile([P, PACK, NQ], F32, name="q_raw", align_bytes=256)

        def words(dram):
            return dram[0].rearrange("p t r -> p (t r)").bitcast(I32)

        k_bytes = pool.tile([P, N], U8, name="k_bytes", align_bytes=256)
        c_bytes = pool.tile([P, N], U8, name="c_bytes", align_bytes=256)
        warm = pool.tile([P, 2], F32, name="warm")
        nc.gpsimd.memset(warm[:, 0:1], 0.0)
        nc.vector.memset(k_plane[:].bitcast(I32), 0)
        nc.vector.memset(c_plane[:TOP, :].bitcast(I32), 0)
        nc.vector.memset(c_bytes[:].bitcast(I32), 0)
        nc.scalar.dma_start(c_plane[TOP:, :].bitcast(I32), c_scales[0].bitcast(I32))
        nc.sync.dma_start(offsets[:], offs)
        nc.sync.dma_start(q_raw[:], qT[0].rearrange("(p j) q -> p j q", j=PACK))
        nc.scalar.activation(warm[:, 1:2], warm[:, 0:1], mybir.ActivationFunctionType.Silu)
        for r in range(2):
            (nc.sync, nc.scalar)[r].dma_start(
                k_plane[64 * r + K_ROW : 64 * r + K_ROW + 8, :].bitcast(I32), k_scales[0, 8 * r : 8 * r + 8, :].bitcast(I32)
            )
        nc.sync.dma_start(k_table[:], words(k_words))
        nc.sync.dma_start(c_table[:, :REACH], words(c_words)[:, :REACH])

        q_grouped = pool.tile([P, NQ, PACK], BF16, name="q_grouped", align_bytes=256)
        q_codes = pool.tile([P, NQ], U32, name="q_codes", tag="k_slot", align_bytes=256)
        q_plane = pool.tile([P, NQ], U8, name="q_plane", align_bytes=256)
        nc.scalar.copy(out=q_grouped[:], in_=q_raw[:].rearrange("p j q -> p q j"))
        c_listed = pool.tile([P, N], U8, name="c_listed", align_bytes=256)
        nc.vector.tensor_copy(c_listed[:], c_plane[:].indirect(offsets[:]))
        k_listed = pool.tile([P, N], U8, name="k_listed", align_bytes=256)
        nc.vector.tensor_copy(k_listed[:], k_plane[:].indirect(offsets[:]))
        nc.vector.tensor_copy(k_bytes[:].bitcast(I32), k_listed[:].bitcast(I32))
        for r in range(2):
            nc.sync.dma_start(
                k_bytes[64 * r + 32 + K_ROW : 64 * r + 36 + K_ROW, :].bitcast(I32),
                k_listed[64 * r + K_ROW + 4 : 64 * r + K_ROW + 8, :].bitcast(I32),
            )
        nc.sync.dma_start(c_table[:, REACH:], words(c_words)[:, REACH:])
        for r in range(4):
            nc.sync.dma_start(c_bytes[r:P:32, :].bitcast(I32), c_listed[TOP + r : P : 4, :].bitcast(I32))
        nc.vector.quantize_mx(
            out=q_codes[:].bitcast(FP8X4), scales=q_plane[:], in_=q_grouped[:].rearrange("p q j -> p (q j)")
        )

        def product(name, table, picked, picked_bytes, row, h):
            cols = slice(h * HALF, (h + 1) * HALF)
            nc.vector.tensor_copy(picked[:, cols], table[:, : (REACH, T)[h]].bitcast(U32).indirect(offsets[:, h * HALF // 16 : (h + 1) * HALF // 16]))
            acc = psum.tile([NQ, HALF], F32, name=name + "_acc%d" % h)
            nc.tensor.matmul_mx(
                out=acc[:],
                lhsT=q_codes[:].bitcast(FP8X4),
                lhsT_scale=q_plane[:],
                rhs=picked[:, cols].bitcast(FP8X4),
                rhs_scale=picked_bytes[row:P, cols],
                start=True,
                stop=True,
            )
            return acc

        gate = pool.tile([NQ, N], F32, name="gate", align_bytes=256)
        k_picked = pool.tile([P, N], U32, name="k_picked", tag="c_slot", align_bytes=256)
        for h in range(2):
            acc = product("k", k_table, k_picked, k_bytes, K_ROW, h)
            nc.scalar.activation(gate[:, h * HALF : (h + 1) * HALF], acc[:], mybir.ActivationFunctionType.Silu)

        c_picked = pool.tile([P, N], U32, name="c_picked", align_bytes=256)
        gathers = ((0, HALF, REACH), (HALF, HALF + QUARTER, T), (HALF + QUARTER, N, T))
        layers = []
        for a, b, reach in gathers:
            nc.vector.tensor_copy(c_picked[:, a:b], c_table[:, :reach].bitcast(U32).indirect(offsets[:, a // 16 : b // 16]))
            for start in range(a, b, QUARTER):
                cols = slice(start, start + QUARTER)
                acc = psum.tile([NQ, QUARTER], F32, name="c_acc%d" % start)
                nc.tensor.matmul_mx(
                    out=acc[:],
                    lhsT=q_codes[:].bitcast(FP8X4),
                    lhsT_scale=q_plane[:],
                    rhs=c_picked[:, cols].bitcast(FP8X4),
                    rhs_scale=c_bytes[:, cols],
                    start=True,
                    stop=True,
                )
                layers.append((cols, acc))
        result = pool.tile([NQ, N], F32, name="result", align_bytes=256)
        cut = QUARTER + QUARTER // 2
        for cols, acc in layers:
            edges = sorted({cols.start, cols.stop} | ({cut} if cols.start < cut < cols.stop else set()))
            for a, b in zip(edges, edges[1:]):
                nc.vector.tensor_tensor(result[:, a:b], acc[:, a - cols.start : b - cols.start], gate[:, a:b], mybir.AluOpType.mult)
        for a, b, queue in ((0, cut, nc.scalar), (cut, N - QUARTER, nc.scalar), (N - QUARTER, N, nc.sync)):
            queue.dma_start(out[0, :, a:b], result[:, a:b])
